import numpy as np, ml_dtypes
CORES = [89,94,345,350]
N = 4
import mx_ref
NC, G = 128, 2
C = np.float32(0.043)
BF = ml_dtypes.bfloat16
def cut(t, i, w=512):
    return t[:, w * i:w * i + w]
def tile(rs):
    return np.stack(rs, axis=2).reshape(128, -1).astype(BF)
def layer(w, X):
    out = []
    for i in range(G):
        for t in range(len(X)):
            p = mx_ref.matmul(mx_ref.quantize(cut(w, len(X) * i + t)), X[t])
            z = p if t == 0 else z + p
        out.append(z)
    return out
def act(Z):
    return [np.maximum(s * z, 0) * C for z in Z for s in (1, -1)]
def pick(b):
    s = np.zeros((128, 128, 4), np.float32)
    s[np.arange(128), np.arange(128), b] = 1.0
    return mx_ref.quantize(s.reshape(128, 512).astype(BF))
def setup_inputs(rng):
    def f(*shape):
        return mx_ref.flush((rng.standard_normal(shape, dtype=np.float32) * np.exp2(rng.integers(-2, 3, shape[:-1] + (1,)))).astype(BF))
    return {"a": f(N, 128, G * 512), "b": f(N, 128, N * 4 * NC)}
def setup_inputs_blocks(rng):
    d = setup_inputs(rng)
    for k in ("a", "b"): d[k] = mx_ref.spread(d[k], rng, 4)
    return d
def setup_inputs_wide(rng):
    d = setup_inputs(rng)
    for k in ("a", "b"): d[k] = mx_ref.flush((d[k].astype(np.float32) * np.exp2(rng.integers(-8, 9, (N, 1, 1))).astype(np.float32)).astype(BF))
    return d
def reference(a, b):
    S = [pick(t) for t in range(4)]
    y = np.zeros((N, 128, NC, 4), np.float32)
    for c in range(N):
        for k in range(1, N + 1):
            r = (c + k) % N
            R = act(layer(a[r], [mx_ref.quantize(cut(b[r], c, 4 * NC))]))
            if k > 1: R = [R[t] + mx_ref.matmul(S[t], q) for t in range(4)]
            if k < N: q = mx_ref.quantize(tile(R))
        y[c] = np.stack(R, axis=2)
    return {"y": y.reshape(N, 128, 4 * NC)}

@@ -1,0 +1,210 @@
+from concourse.mybir import dt, AluOpType, ActivationFunctionType
+
+N = 4
+NC = 128
+W = 4 * NC
+CS = 0.043
+WORLD = 512
+BANK = 512
+
+SCRATCH = {
+    "a_t": ("sbuf", [128, 2 * W], "bfloat16"),
+    "b_t": ("sbuf", [128, N * W], "bfloat16"),
+    "s_t": ("sbuf", [128, 4 * W], "bfloat16"),
+    "idx": ("sbuf", [128, NC], "float32"),
+    "qa": ("sbuf", [128, 2 * NC], "float8_e4m3fn_x4"), "pa": ("sbuf", [128, 2 * NC], "uint8"),
+    "qb": ("sbuf", [128, N * NC], "float8_e4m3fn_x4"), "pb": ("sbuf", [128, N * NC], "uint8"),
+    "qs": ("sbuf", [128, 4 * NC], "float8_e4m3fn_x4"), "ps": ("sbuf", [128, 4 * NC], "uint8"),
+    "part": ("sbuf", [128, 3 * W], "float32"),
+    "h": ("sbuf", [128, 3 * W], "bfloat16"),
+    "qh": ("sbuf", [128, 3 * NC], "float8_e4m3fn_x4"), "ph": ("sbuf", [128, 3 * NC], "uint8"),
+    "qi": ("sbuf", [128, 3 * NC], "float8_e4m3fn_x4"), "pi": ("sbuf", [128, 3 * NC], "uint8"),
+    "yt": ("sbuf", [128, W], "float32"),
+    "acc": ("psum", [128, 8 * BANK], "float32"),
+}
+SEMAPHORES = (["ld_a", "ld_b", "ld_r", "iot", "zer", "one", "q_b", "q_a0", "q_a1", "z_0", "z_1", "act", "q_s", "q_r",
+               "zr_0", "zr_1", "actr", "sent", "st"]
+              + ["q_h%d" % k for k in range(3)] + ["arr%d" % k for k in range(3)] + ["add%d" % k for k in range(3)]
+              + ["d%d_%d" % (s, b) for s in range(3) for b in range(4)])
+
+
+def _engines(mask):
+    return bin(mask).count("1")
+
+
+def _relays(topo, src, dst, group):
+    far, near = None, None
+    for x in range(WORLD):
+        if x in group or topo.host(x) in (topo.host(src), topo.host(dst)):
+            continue
+        if topo.chip(x) != topo.chip(src) or topo.chip(x) != topo.chip(dst):
+            continue
+        if not (topo.may_write(src, x) and topo.may_write(x, dst)):
+            continue
+        cable_first = topo.rack(topo.host(x)) != topo.rack(topo.host(src))
+        if topo.die(x) != topo.die(src if cable_first else dst):
+            continue
+        if cable_first and far is None:
+            far = x
+        if not cable_first and near is None:
+            near = x
+    return far, near
+
+
+def _flows(T, topo):
+    cores = list(T.cores)
+    out = []
+    for r in range(N):
+        src, dst = cores[r], cores[(r + 1) % N]
+        if topo.may_write(src, dst):
+            out.append((src, dst, None, None))
+        else:
+            far, near = _relays(topo, src, dst, cores)
+            out.append((src, dst, far, near))
+    return out
+
+
+def _codes(buf, k):
+    return buf[:, NC * k:NC * (k + 1)].bitcast(dt.uint8)
+
+
+def _plane(buf, k):
+    return buf[:, NC * k:NC * (k + 1)]
+
+
+def _write(g, T, topo, core, to, out_ap, in_ap, k):
+    rid, pid = topo.addr(to, core)
+    mask = topo.mask(core, to)
+    g.remote_dma(out_ap=out_ap, in_ap=in_ap, remote_sem=T.sem["arr%d" % k], local_sem=T.sem.sent,
+                 pid=pid, routing_id=rid, dma_engine_mask=mask)
+    return _engines(mask)
+
+
+def _relay(g, core, T, topo, src, dst, codes):
+    left = 0
+    for k in range(3):
+        g.wait_ge(T.sem["arr%d" % k], _engines(topo.mask(src, core)))
+        if codes:
+            left += _write(g, T, topo, core, dst, _codes(T.qi, k), _codes(T.qi, k), k)
+        else:
+            left += _write(g, T, topo, core, dst, _plane(T.pi, k), _plane(T.pi, k), k)
+    g.wait_ge(T.sem.sent, left)
+
+
+def rank_program(g, core, T, topo):
+    flows = _flows(T, topo)
+    r = T.rank_of(core)
+    if r is None:
+        for (src, dst, by_c, by_p) in flows:
+            if core == by_c:
+                _relay(g, core, T, topo, src, dst, True)
+            elif core == by_p:
+                _relay(g, core, T, topo, src, dst, False)
+        return
+
+    S = T.sem
+    v, te, sc, sy = g.vector, g.tensor, g.scalar, g.sync
+    mult, vmax, add = AluOpType.mult, AluOpType.max, AluOpType.add
+    relu = ActivationFunctionType.Relu
+
+    def bank(i, n):
+        return T.acc[:, BANK * i:BANK * i + n]
+
+    def a_side(i):
+        return T.qa[:, NC * i:NC * (i + 1)], T.pa[:, NC * i:NC * (i + 1)]
+
+    (p_src, _, p_c, p_p) = flows[(r - 1) % N]
+    landed = _engines(topo.mask(p_c if p_c is not None else p_src, core)) \
+        + _engines(topo.mask(p_p if p_p is not None else p_src, core))
+    (_, nxt, by_c, by_p) = flows[r]
+    to_c = by_c if by_c is not None else nxt
+    to_p = by_p if by_p is not None else nxt
+
+    c0 = (r - 1) % N
+    sy.dma_start(T.a_t[:], T.a[:]).then_inc(S.ld_a, 16)
+    sc.dma_start(T.b_t[:, 0:W], T.b[:, W * c0:W * (c0 + 1)]).then_inc(S.ld_b, 16)
+    sy.wait_ge(S.ld_a, 16)
+    sy.wait_ge(S.ld_b, 16)
+    i, rest = 0, 0
+    while i < 3:
+        c = (r + i) % N
+        n = min(3 - i, N - c)
+        sy.dma_start(T.b_t[:, W * (1 + i):W * (1 + i + n)], T.b[:, W * c:W * (c + n)]).then_inc(S.ld_r, 16)
+        i += n
+        rest += 16
+
+    g.iota(T.idx[:], [[1, NC]], 0, -1, allow_small_or_imprecise_dtypes=True).then_inc(S.iot, 1)
+    left = 0
+    for k in range(3):
+        g.wait_ge(S["q_h%d" % k], 1)
+        left += _write(g, T, topo, core, to_c, _codes(T.qi, k), _codes(T.qh, k), k)
+        left += _write(g, T, topo, core, to_p, _plane(T.pi, k), _plane(T.ph, k), k)
+    g.wait_ge(S.sent, left)
+
+    te.wait_ge(S.q_b, 1)
+    for i in range(2):
+        te.wait_ge(S["q_a%d" % i], 1)
+        qa, pa = a_side(i)
+        te.matmul_mx(bank(i, NC), qa, pa, T.qb[:, 0:NC], T.pb[:, 0:NC], True, True).then_inc(S["z_%d" % i], 1)
+    te.wait_ge(S.q_r, 1)
+    for i in range(2):
+        qa, pa = a_side(i)
+        te.matmul_mx(bank(2 + i, 3 * NC), qa, pa, T.qb[:, NC:N * NC], T.pb[:, NC:N * NC], True, True).then_inc(S["zr_%d" % i], 1)
+    te.wait_ge(S.q_s, 1)
+    first = [4, 0, 4]
+    for s in range(3):
+        if s == 1:
+            te.wait_ge(S.act, 4)
+            te.wait_ge(S.actr, 4)
+        if s == 2:
+            te.wait_ge(S.add0, 4)
+        te.wait_ge(S["arr%d" % s], landed)
+        for b in range(4):
+            te.matmul_mx(bank(first[s] + b, NC), T.qs[:, NC * b:NC * (b + 1)], T.ps[:, NC * b:NC * (b + 1)],
+                         T.qi[:, NC * s:NC * (s + 1)], T.pi[:, NC * s:NC * (s + 1)], True, True).then_inc(S["d%d_%d" % (s, b)], 1)
+
+    sc.wait_ge(S.z_0, 1)
+    sc.activation(T.h[:, 0:W:4], bank(0, NC), relu, scale=CS).then_inc(S.act, 1)
+    sc.activation(T.h[:, 1:W:4], bank(0, NC), relu, scale=-CS).then_inc(S.act, 1)
+    sc.wait_ge(S.zr_0, 1)
+    sc.activation(T.part[:, 0:3 * W:4], bank(2, 3 * NC), relu, scale=CS).then_inc(S.actr, 1)
+    sc.activation(T.part[:, 1:3 * W:4], bank(2, 3 * NC), relu, scale=-CS).then_inc(S.actr, 1)
+
+    v.memset(T.s_t[:], 0.0).then_inc(S.zer, 1)
+    v.wait_ge(S.ld_b, 16)
+    v.quantize_mx(T.qb[:, 0:NC], T.pb[:, 0:NC], T.b_t[:, 0:W]).then_inc(S.q_b, 1)
+    v.wait_ge(S.ld_a, 16)
+    for i in range(2):
+        qa, pa = a_side(i)
+        v.quantize_mx(qa, pa, T.a_t[:, W * i:W * (i + 1)]).then_inc(S["q_a%d" % i], 1)
+    v.wait_ge(S.z_1, 1)
+    v.tensor_scalar(T.h[:, 2:W:4], bank(1, NC), CS, 0.0, mult, vmax).then_inc(S.act, 1)
+    v.tensor_scalar(T.h[:, 3:W:4], bank(1, NC), -CS, 0.0, mult, vmax).then_inc(S.act, 1)
+    v.wait_ge(S.act, 4)
+    v.quantize_mx(T.qh[:, 0:NC], T.ph[:, 0:NC], T.h[:, 0:W]).then_inc(S.q_h0, 1)
+    v.wait_ge(S.zer, 1)
+    v.wait_ge(S.iot, 1)
+    for b in range(4):
+        v.tensor_scalar(T.s_t[:, W * b + b:W * (b + 1):4], T.idx[:], 0.0, None, AluOpType.is_equal).then_inc(S.one, 1)
+    v.wait_ge(S.one, 4)
+    v.quantize_mx(T.qs[:], T.ps[:], T.s_t[:]).then_inc(S.q_s, 1)
+    v.wait_ge(S.ld_r, rest)
+    v.quantize_mx(T.qb[:, NC:N * NC], T.pb[:, NC:N * NC], T.b_t[:, W:N * W]).then_inc(S.q_r, 1)
+    v.wait_ge(S.zr_1, 1)
+    v.tensor_scalar(T.part[:, 2:3 * W:4], bank(3, 3 * NC), CS, 0.0, mult, vmax).then_inc(S.actr, 1)
+    v.tensor_scalar(T.part[:, 3:3 * W:4], bank(3, 3 * NC), -CS, 0.0, mult, vmax).then_inc(S.actr, 1)
+    v.wait_ge(S.actr, 4)
+    for s in range(3):
+        i = 2 - s
+        for b in range(4):
+            v.wait_ge(S["d%d_%d" % (s, b)], 1)
+            out = T.h[:, W * (s + 1) + b:W * (s + 2):4] if s < 2 else T.yt[:, b:W:4]
+            v.tensor_tensor(out, T.part[:, W * i + b:W * (i + 1):4], bank(first[s] + b, NC), add).then_inc(S["add%d" % s], 1)
+        if s < 2:
+            v.wait_ge(S["add%d" % s], 4)
+            v.quantize_mx(T.qh[:, NC * (s + 1):NC * (s + 2)], T.ph[:, NC * (s + 1):NC * (s + 2)],
+                          T.h[:, W * (s + 1):W * (s + 2)]).then_inc(S["q_h%d" % (s + 1)], 1)
+
+    sy.wait_ge(S.add2, 4)
+    sy.dma_start(T.y[:], T.yt[:]).then_inc(S.st, 16)
+    sy.wait_ge(S.st, 16)

@@ -32,44 +32,44 @@ def _engines(mask):
     return bin(mask).count("1")
 
 
-def _relays(topo, src, dst, group):
-    far, near = None, None
+def _find(topo, src, dst, used, far, die):
     for x in range(WORLD):
-        if x in group or topo.host(x) in (topo.host(src), topo.host(dst)):
+        if x in used or topo.host(x) in (topo.host(src), topo.host(dst)):
             continue
         if topo.chip(x) != topo.chip(src) or topo.chip(x) != topo.chip(dst):
             continue
         if not (topo.may_write(src, x) and topo.may_write(x, dst)):
             continue
-        cable_first = topo.rack(topo.host(x)) != topo.rack(topo.host(src))
-        if topo.die(x) != topo.die(src if cable_first else dst):
+        if (topo.rack(topo.host(x)) != topo.rack(topo.host(src))) != far or topo.die(x) != die:
             continue
-        if cable_first and far is None:
-            far = x
-        if not cable_first and near is None:
-            near = x
-    return far, near
+        used.add(x)
+        return x
+    return None
 
 
 def _flows(T, topo):
     cores = list(T.cores)
+    used = set(cores)
     out = []
     for r in range(N):
         src, dst = cores[r], cores[(r + 1) % N]
         if topo.may_write(src, dst):
-            out.append((src, dst, None, None))
-        else:
-            far, near = _relays(topo, src, dst, cores)
-            out.append((src, dst, far, near))
+            out.append((src, dst, [(True, 0, NC, None), (False, 0, NC, None)]))
+            continue
+        other = [d for d in (topo.die(x) for x in range(WORLD)) if d != topo.die(dst)][0]
+        out.append((src, dst, [
+            (True, 0, NC // 2, _find(topo, src, dst, used, True, topo.die(src))),
+            (True, NC // 2, NC, _find(topo, src, dst, used, False, topo.die(dst))),
+            (False, 0, NC, _find(topo, src, dst, used, False, other)),
+        ]))
     return out
 
 
-def _codes(buf, k):
-    return buf[:, NC * k:NC * (k + 1)].bitcast(dt.uint8)
-
-
-def _plane(buf, k):
-    return buf[:, NC * k:NC * (k + 1)]
+def _view(T, arrive, piece, k):
+    codes, c0, c1, _ = piece
+    if codes:
+        return (T.qi if arrive else T.qh)[:, NC * k + c0:NC * k + c1].bitcast(dt.uint8)
+    return (T.pi if arrive else T.ph)[:, NC * k + c0:NC * k + c1]
 
 
 def _write(g, T, topo, core, to, out_ap, in_ap, k):
@@ -80,14 +80,11 @@ def _write(g, T, topo, core, to, out_ap, in_ap, k):
     return _engines(mask)
 
 
-def _relay(g, core, T, topo, src, dst, codes):
+def _relay(g, core, T, topo, src, dst, piece):
     left = 0
     for k in range(3):
         g.wait_ge(T.sem["arr%d" % k], _engines(topo.mask(src, core)))
-        if codes:
-            left += _write(g, T, topo, core, dst, _codes(T.qi, k), _codes(T.qi, k), k)
-        else:
-            left += _write(g, T, topo, core, dst, _plane(T.pi, k), _plane(T.pi, k), k)
+        left += _write(g, T, topo, core, dst, _view(T, True, piece, k), _view(T, True, piece, k), k)
     g.wait_ge(T.sem.sent, left)
 
 
@@ -95,11 +92,10 @@ def rank_program(g, core, T, topo):
     flows = _flows(T, topo)
     r = T.rank_of(core)
     if r is None:
-        for (src, dst, by_c, by_p) in flows:
-            if core == by_c:
-                _relay(g, core, T, topo, src, dst, True)
-            elif core == by_p:
-                _relay(g, core, T, topo, src, dst, False)
+        for (src, dst, pieces) in flows:
+            for piece in pieces:
+                if core == piece[3]:
+                    _relay(g, core, T, topo, src, dst, piece)
         return
 
     S = T.sem
@@ -113,12 +109,9 @@ def rank_program(g, core, T, topo):
     def a_side(i):
         return T.qa[:, NC * i:NC * (i + 1)], T.pa[:, NC * i:NC * (i + 1)]
 
-    (p_src, _, p_c, p_p) = flows[(r - 1) % N]
-    landed = _engines(topo.mask(p_c if p_c is not None else p_src, core)) \
-        + _engines(topo.mask(p_p if p_p is not None else p_src, core))
-    (_, nxt, by_c, by_p) = flows[r]
-    to_c = by_c if by_c is not None else nxt
-    to_p = by_p if by_p is not None else nxt
+    (p_src, _, p_pieces) = flows[(r - 1) % N]
+    landed = sum(_engines(topo.mask(p[3] if p[3] is not None else p_src, core)) for p in p_pieces)
+    (_, nxt, pieces) = flows[r]
 
     c0 = (r - 1) % N
     sy.dma_start(T.a_t[:], T.a[:]).then_inc(S.ld_a, 16)
@@ -137,8 +130,9 @@ def rank_program(g, core, T, topo):
     left = 0
     for k in range(3):
         g.wait_ge(S["q_h%d" % k], 1)
-        left += _write(g, T, topo, core, to_c, _codes(T.qi, k), _codes(T.qh, k), k)
-        left += _write(g, T, topo, core, to_p, _plane(T.pi, k), _plane(T.ph, k), k)
+        for piece in pieces:
+            to = piece[3] if piece[3] is not None else nxt
+            left += _write(g, T, topo, core, to, _view(T, True, piece, k), _view(T, False, piece, k), k)
     g.wait_ge(S.sent, left)
 
     te.wait_ge(S.q_b, 1)

from concourse.mybir import dt, AluOpType, ActivationFunctionType

N = 4
NC = 128
W = 4 * NC
CS = 0.043
WORLD = 512
BANK = 512

SCRATCH = {
    "a_t": ("sbuf", [128, 2 * W], "bfloat16"),
    "b_t": ("sbuf", [128, N * W], "bfloat16"),
    "s_t": ("sbuf", [128, 4 * W], "bfloat16"),
    "idx": ("sbuf", [128, NC], "float32"),
    "qa": ("sbuf", [128, 2 * NC], "float8_e4m3fn_x4"), "pa": ("sbuf", [128, 2 * NC], "uint8"),
    "qb": ("sbuf", [128, N * NC], "float8_e4m3fn_x4"), "pb": ("sbuf", [128, N * NC], "uint8"),
    "qs": ("sbuf", [128, 4 * NC], "float8_e4m3fn_x4"), "ps": ("sbuf", [128, 4 * NC], "uint8"),
    "part": ("sbuf", [128, 3 * W], "float32"),
    "h": ("sbuf", [128, 3 * W], "bfloat16"),
    "qh": ("sbuf", [128, 3 * NC], "float8_e4m3fn_x4"), "ph": ("sbuf", [128, 3 * NC], "uint8"),
    "qi": ("sbuf", [128, 3 * NC], "float8_e4m3fn_x4"), "pi": ("sbuf", [128, 3 * NC], "uint8"),
    "yt": ("sbuf", [128, W], "float32"),
    "acc": ("psum", [128, 8 * BANK], "float32"),
}
SEMAPHORES = (["ld_a", "ld_b", "ld_r", "iot", "zer", "one", "q_b", "q_a0", "q_a1", "z_0", "z_1", "act", "q_s", "q_r",
               "zr_0", "zr_1", "actr", "sent", "st"]
              + ["q_h%d" % k for k in range(3)] + ["arr%d" % k for k in range(3)] + ["add%d" % k for k in range(3)]
              + ["d%d_%d" % (s, b) for s in range(3) for b in range(4)])


def _engines(mask):
    return bin(mask).count("1")


def _find(topo, src, dst, used, far, die):
    for x in range(WORLD):
        if x in used or topo.host(x) in (topo.host(src), topo.host(dst)):
            continue
        if topo.chip(x) != topo.chip(src) or topo.chip(x) != topo.chip(dst):
            continue
        if not (topo.may_write(src, x) and topo.may_write(x, dst)):
            continue
        if (topo.rack(topo.host(x)) != topo.rack(topo.host(src))) != far or topo.die(x) != die:
            continue
        used.add(x)
        return x
    return None


def _flows(T, topo):
    cores = list(T.cores)
    used = set(cores)
    out = []
    for r in range(N):
        src, dst = cores[r], cores[(r + 1) % N]
        if topo.may_write(src, dst):
            out.append((src, dst, [(True, 0, NC, None), (False, 0, NC, None)]))
            continue
        other = [d for d in (topo.die(x) for x in range(WORLD)) if d != topo.die(dst)][0]
        out.append((src, dst, [
            (True, 0, NC // 2, _find(topo, src, dst, used, True, topo.die(src))),
            (True, NC // 2, NC, _find(topo, src, dst, used, False, topo.die(dst))),
            (False, 0, NC, _find(topo, src, dst, used, False, other)),
        ]))
    return out


def _view(T, arrive, piece, k):
    codes, c0, c1, _ = piece
    if codes:
        return (T.qi if arrive else T.qh)[:, NC * k + c0:NC * k + c1].bitcast(dt.uint8)
    return (T.pi if arrive else T.ph)[:, NC * k + c0:NC * k + c1]


def _write(g, T, topo, core, to, out_ap, in_ap, k):
    rid, pid = topo.addr(to, core)
    mask = topo.mask(core, to)
    g.remote_dma(out_ap=out_ap, in_ap=in_ap, remote_sem=T.sem["arr%d" % k], local_sem=T.sem.sent,
                 pid=pid, routing_id=rid, dma_engine_mask=mask)
    return _engines(mask)


def _relay(g, core, T, topo, src, dst, piece):
    left = 0
    for k in range(3):
        g.wait_ge(T.sem["arr%d" % k], _engines(topo.mask(src, core)))
        left += _write(g, T, topo, core, dst, _view(T, True, piece, k), _view(T, True, piece, k), k)
    g.wait_ge(T.sem.sent, left)


def rank_program(g, core, T, topo):
    flows = _flows(T, topo)
    r = T.rank_of(core)
    if r is None:
        for (src, dst, pieces) in flows:
            for piece in pieces:
                if core == piece[3]:
                    _relay(g, core, T, topo, src, dst, piece)
        return

    S = T.sem
    v, te, sc, sy = g.vector, g.tensor, g.scalar, g.sync
    mult, vmax, add = AluOpType.mult, AluOpType.max, AluOpType.add
    relu = ActivationFunctionType.Relu

    def bank(i, n):
        return T.acc[:, BANK * i:BANK * i + n]

    def a_side(i):
        return T.qa[:, NC * i:NC * (i + 1)], T.pa[:, NC * i:NC * (i + 1)]

    (p_src, _, p_pieces) = flows[(r - 1) % N]
    landed = sum(_engines(topo.mask(p[3] if p[3] is not None else p_src, core)) for p in p_pieces)
    (_, nxt, pieces) = flows[r]

    c0 = (r - 1) % N
    sy.dma_start(T.a_t[:], T.a[:]).then_inc(S.ld_a, 16)
    sc.dma_start(T.b_t[:, 0:W], T.b[:, W * c0:W * (c0 + 1)]).then_inc(S.ld_b, 16)
    sy.wait_ge(S.ld_a, 16)
    sy.wait_ge(S.ld_b, 16)
    i, rest = 0, 0
    while i < 3:
        c = (r + i) % N
        n = min(3 - i, N - c)
        sy.dma_start(T.b_t[:, W * (1 + i):W * (1 + i + n)], T.b[:, W * c:W * (c + n)]).then_inc(S.ld_r, 16)
        i += n
        rest += 16

    g.iota(T.idx[:], [[1, NC]], 0, -1, allow_small_or_imprecise_dtypes=True).then_inc(S.iot, 1)
    left = 0
    for k in range(3):
        g.wait_ge(S["q_h%d" % k], 1)
        for piece in pieces:
            to = piece[3] if piece[3] is not None else nxt
            left += _write(g, T, topo, core, to, _view(T, True, piece, k), _view(T, False, piece, k), k)
    g.wait_ge(S.sent, left)

    te.wait_ge(S.q_b, 1)
    for i in range(2):
        te.wait_ge(S["q_a%d" % i], 1)
        qa, pa = a_side(i)
        te.matmul_mx(bank(i, NC), qa, pa, T.qb[:, 0:NC], T.pb[:, 0:NC], True, True).then_inc(S["z_%d" % i], 1)
    te.wait_ge(S.q_r, 1)
    for i in range(2):
        qa, pa = a_side(i)
        te.matmul_mx(bank(2 + i, 3 * NC), qa, pa, T.qb[:, NC:N * NC], T.pb[:, NC:N * NC], True, True).then_inc(S["zr_%d" % i], 1)
    te.wait_ge(S.q_s, 1)
    first = [4, 0, 4]
    for s in range(3):
        if s == 1:
            te.wait_ge(S.act, 4)
            te.wait_ge(S.actr, 4)
        if s == 2:
            te.wait_ge(S.add0, 4)
        te.wait_ge(S["arr%d" % s], landed)
        for b in range(4):
            te.matmul_mx(bank(first[s] + b, NC), T.qs[:, NC * b:NC * (b + 1)], T.ps[:, NC * b:NC * (b + 1)],
                         T.qi[:, NC * s:NC * (s + 1)], T.pi[:, NC * s:NC * (s + 1)], True, True).then_inc(S["d%d_%d" % (s, b)], 1)

    sc.wait_ge(S.z_0, 1)
    sc.activation(T.h[:, 0:W:4], bank(0, NC), relu, scale=CS).then_inc(S.act, 1)
    sc.activation(T.h[:, 1:W:4], bank(0, NC), relu, scale=-CS).then_inc(S.act, 1)
    sc.wait_ge(S.zr_0, 1)
    sc.activation(T.part[:, 0:3 * W:4], bank(2, 3 * NC), relu, scale=CS).then_inc(S.actr, 1)
    sc.activation(T.part[:, 1:3 * W:4], bank(2, 3 * NC), relu, scale=-CS).then_inc(S.actr, 1)

    v.memset(T.s_t[:], 0.0).then_inc(S.zer, 1)
    v.wait_ge(S.ld_b, 16)
    v.quantize_mx(T.qb[:, 0:NC], T.pb[:, 0:NC], T.b_t[:, 0:W]).then_inc(S.q_b, 1)
    v.wait_ge(S.ld_a, 16)
    for i in range(2):
        qa, pa = a_side(i)
        v.quantize_mx(qa, pa, T.a_t[:, W * i:W * (i + 1)]).then_inc(S["q_a%d" % i], 1)
    v.wait_ge(S.z_1, 1)
    v.tensor_scalar(T.h[:, 2:W:4], bank(1, NC), CS, 0.0, mult, vmax).then_inc(S.act, 1)
    v.tensor_scalar(T.h[:, 3:W:4], bank(1, NC), -CS, 0.0, mult, vmax).then_inc(S.act, 1)
    v.wait_ge(S.act, 4)
    v.quantize_mx(T.qh[:, 0:NC], T.ph[:, 0:NC], T.h[:, 0:W]).then_inc(S.q_h0, 1)
    v.wait_ge(S.zer, 1)
    v.wait_ge(S.iot, 1)
    for b in range(4):
        v.tensor_scalar(T.s_t[:, W * b + b:W * (b + 1):4], T.idx[:], 0.0, None, AluOpType.is_equal).then_inc(S.one, 1)
    v.wait_ge(S.one, 4)
    v.quantize_mx(T.qs[:], T.ps[:], T.s_t[:]).then_inc(S.q_s, 1)
    v.wait_ge(S.ld_r, rest)
    v.quantize_mx(T.qb[:, NC:N * NC], T.pb[:, NC:N * NC], T.b_t[:, W:N * W]).then_inc(S.q_r, 1)
    v.wait_ge(S.zr_1, 1)
    v.tensor_scalar(T.part[:, 2:3 * W:4], bank(3, 3 * NC), CS, 0.0, mult, vmax).then_inc(S.actr, 1)
    v.tensor_scalar(T.part[:, 3:3 * W:4], bank(3, 3 * NC), -CS, 0.0, mult, vmax).then_inc(S.actr, 1)
    v.wait_ge(S.actr, 4)
    for s in range(3):
        i = 2 - s
        for b in range(4):
            v.wait_ge(S["d%d_%d" % (s, b)], 1)
            out = T.h[:, W * (s + 1) + b:W * (s + 2):4] if s < 2 else T.yt[:, b:W:4]
            v.tensor_tensor(out, T.part[:, W * i + b:W * (i + 1):4], bank(first[s] + b, NC), add).then_inc(S["add%d" % s], 1)
        if s < 2:
            v.wait_ge(S["add%d" % s], 4)
            v.quantize_mx(T.qh[:, NC * (s + 1):NC * (s + 2)], T.ph[:, NC * (s + 1):NC * (s + 2)],
                          T.h[:, W * (s + 1):W * (s + 2)]).then_inc(S["q_h%d" % (s + 1)], 1)

    sy.wait_ge(S.add2, 4)
    sy.dma_start(T.y[:], T.yt[:]).then_inc(S.st, 16)
    sy.wait_ge(S.st, 16)
